import numpy as np
import ml_dtypes


def mxq(x, axis, fmt="e4m3"):
    dtype, down = {"e4m3": (ml_dtypes.float8_e4m3fn, 7), "e5m2": (ml_dtypes.float8_e5m2, 14)}[fmt]
    v = np.moveaxis(np.asarray(x, np.float32).astype(ml_dtypes.bfloat16).astype(np.float64), axis, -1)
    blocks = v.reshape(v.shape[:-1] + (-1, 32))
    amax = np.abs(blocks).max(-1, keepdims=True)
    byte = np.maximum(np.where(amax > 0, np.frexp(amax)[1] - 1 + 127, 0) - down, 1)
    scale = np.exp2(byte - 127.0)
    codes = (blocks / scale).astype(np.float32).astype(dtype).astype(np.float64)
    return np.moveaxis((codes * scale).reshape(v.shape), -1, axis)


WIDE = False


def mx_kscale(k):
    if not WIDE:
        return np.ones(k)
    levels = np.array([10, -10, 5, -5, 0])
    if k % 512:
        return np.exp2(np.random.permutation(np.resize(levels, k // 32))).repeat(32)
    a = np.empty((k // 512, 16))
    for p in range(k // 512):
        a[p, :8] = np.random.permutation(np.resize(levels, 8))
        for g in range(8):
            far = levels[np.abs(levels - a[p, g]) >= 10]
            a[p, g + 8] = far[np.random.randint(len(far))]
    return np.exp2(a.ravel()).repeat(32)


def f64(x):
    return np.asarray(x).astype(np.float64)


def striped(idx):
    return np.tile(idx.reshape(-1, 16).T, (8, 1)).astype(np.uint16)


def unstriped(offs):
    return offs[:16].T.reshape(-1).astype(np.int64)


def striped8(idx):
    return np.concatenate([x.reshape(-1, 16).T for x in idx]).astype(np.uint16)


def runs(offs, k):
    lists = np.stack([offs[16 * r : 16 * r + 16].T.reshape(-1) for r in range(8)]).astype(np.int64)
    return lists[np.arange(k) % 512 // 64]


def pack_weight(w):
    k, n = w.shape
    w = f64(np.asarray(w, np.float32).astype(ml_dtypes.bfloat16)).reshape(k // 32, 32, n)
    amax = np.abs(w).max(1)
    byte = np.clip(np.where(amax > 0, np.frexp(amax)[1] - 1 + 127 - 7, 1), 1, 254)
    scaled = (w * np.exp2(127.0 - byte)[:, None, :]).reshape(k, n).astype(np.float32)
    words = np.ascontiguousarray(scaled.reshape(k // 512, 128, 4, n).transpose(0, 1, 3, 2)).astype(ml_dtypes.float8_e4m3fn).view(np.uint8)
    return words, np.ascontiguousarray(byte.astype(np.uint8).reshape(k // 512, 16, n))


def unpack_weight(words, scales):
    g, p, n, _ = words.shape
    vals = np.ascontiguousarray(words).view(ml_dtypes.float8_e4m3fn).astype(np.float64) * np.repeat(np.exp2(scales.astype(np.float64) - 127.0), 8, axis=1)[..., None]
    return vals.transpose(0, 1, 3, 2).reshape(g * 512, n)


def relu(v):
    return np.maximum(v, 0.0)

def planes(y):
    n, m = y.shape
    v = y.astype(np.float32).astype(ml_dtypes.bfloat16).astype(np.float64).reshape(n // 32, 32, m)
    top = np.abs(v).max(1)
    byte = np.clip(np.where(top > 0, np.frexp(top)[1] - 1 + 127 - 7, 1), 1, 254)
    codes = (v * np.exp2(127.0 - byte)[:, None, :]).reshape(n, m).astype(np.float32).astype(ml_dtypes.float8_e4m3fn).view(np.uint8)
    words = codes.reshape(n // 512, 128, 4, m).transpose(0, 1, 3, 2)
    return np.ascontiguousarray(words), np.ascontiguousarray(byte.astype(np.uint8).reshape(n // 512, 16, m))


K, T, S, N, H, U = 512, 2048, 512, 512, 512, 512


def setup_inputs():
    n = np.random.standard_normal
    s = mx_kscale(K)[:, None]
    u = mx_kscale(H)
    packed_xT = pack_weight(n((K, T)) * s)
    packed_w1 = pack_weight(n((K, H)) / np.sqrt(K) / s)
    packed_w2 = pack_weight(n((H, N)) / np.sqrt(H) / u[:, None])
    return {
        "x_words": packed_xT[0],
        "x_scales": packed_xT[1],
        "w1_words": packed_w1[0],
        "w1_scales": packed_w1[1],
        "tab": np.random.uniform(0.1, 0.8, (H, U)).astype(np.float32),
        "gn": (np.random.uniform(0.5, 1.5, (H, 1)) * u[:, None]).astype(np.float32),
        "w2_words": packed_w2[0],
        "w2_scales": packed_w2[1],
        "res": (2 * n((N, S))).astype(np.float32),
        "offs": striped(np.random.permutation(T)[:S]),
        "kind": striped8(np.random.randint(0, U, (8, S))),
        "nb": striped8(np.stack([np.random.permutation(S) for _ in range(8)])),
    }


def reference(x_words, x_scales, w1_words, w1_scales, tab, gn, w2_words, w2_scales, res, offs, kind, nb):
    xq = unpack_weight(x_words, x_scales)[:, unstriped(offs)]
    y = unpack_weight(w1_words, w1_scales).T @ xq
    d = y - (y[np.arange(H)[:, None], runs(nb, H)])
    th = f64(tab)[np.arange(H)[:, None], runs(kind, H)]
    z = f64(gn) * (relu(d - th) - relu(-1.0 * d - th))
    out_0 = f64(res) + (unpack_weight(w2_words, w2_scales).T @ mxq(z, 0, "e4m3"))
    return (out_0,) + planes(out_0)

@@ -1,0 +1,201 @@
+from contextlib import ExitStack
+
+import concourse.mybir as mybir
+
+F32 = mybir.dt.float32
+BF16 = mybir.dt.bfloat16
+I32 = mybir.dt.int32
+U32 = mybir.dt.uint32
+U16 = mybir.dt.uint16
+U8 = mybir.dt.uint8
+FP8X4 = mybir.dt.float8_e4m3fn_x4
+ALU = mybir.AluOpType
+ACT = mybir.ActivationFunctionType
+
+P = 128
+PACK = 4
+T = 2048
+S = 512
+H = 512
+QUADS = 4
+HALF = S // 2
+CHUNKS = (256, 128, 128)
+BANK = 512
+FLOPS = 2 * 2 * 512 * 512 * 512
+
+
+def as_words(words):
+    return words[0].rearrange("p n t -> p (n t)").bitcast(I32)
+
+
+def load_scale_rows(queues, plane, scales):
+    for q, queue in enumerate(queues):
+        queue.dma_start(out=plane[32 * q : 32 * q + 4, :].bitcast(I32), in_=scales[0, 4 * q : 4 * q + 4, :].bitcast(I32))
+
+
+def deal(nc, dst, src, t0, t1):
+    nc.vector.tensor_copy(out=dst[:, t0:t1, :], in_=src[:].rearrange("p (m t) -> p t m", t=PACK)[:, t0:t1, :])
+
+
+def tile_picked_softthr_none_po_kernel(
+    tc, x_words, x_scales, w1_words, w1_scales, tab, gn, w2_words, w2_scales, res, offs, kind, nb, out_0, out_1, out_2
+):
+    nc = tc.nc
+    with ExitStack() as ctx:
+        keep = ctx.enter_context(tc.tile_pool(name="keep", bufs=1))
+        psum = ctx.enter_context(tc.psum_pool(name="psum", bufs=8))
+
+        offs_sb = keep.tile([P, S // 16], U16, name="offs_sb")
+        kind_sb = keep.tile([P, S // 16], U16, name="kind_sb")
+        nb_sb = keep.tile([P, S // 16], U16, name="nb_sb")
+        x_w = keep.tile([P, T], I32, name="x_w", align_bytes=64)
+        x_s = keep.tile([P, T], U8, name="x_s", align_bytes=64)
+        w1_w = keep.tile([P, H], I32, name="w1_w", align_bytes=64)
+        w1_s = keep.tile([P, H], U8, name="w1_s", tag="early", align_bytes=64)
+        w2_w = keep.tile([P, H], I32, name="w2_w", align_bytes=64)
+        w2_s = keep.tile([P, H], U8, name="w2_s", align_bytes=64)
+        gain = keep.tile([P, PACK], F32, name="gain")
+        gain_abs = keep.tile([P, PACK], F32, name="gain_abs")
+        tab_raw = [keep.tile([P, H], F32, name="tab_raw%d" % t, tag="tab_raw%d" % t, align_bytes=64) for t in range(PACK)]
+        res_sb = [keep.tile([P, PACK, n], F32, name="res_sb%d" % c) for c, n in enumerate(CHUNKS)]
+        z_s = keep.tile([P, S], U8, name="z_s", align_bytes=64)
+
+        starts = [sum(CHUNKS[:c]) for c in range(len(CHUNKS))]
+        nc.vector.memset(x_s[:].bitcast(I32), 0)
+        nc.vector.memset(w1_s[:].bitcast(I32), 0)
+        nc.vector.memset(w2_s[:].bitcast(I32), 0)
+        nc.vector.memset(z_s[:].bitcast(I32), 0)
+        nc.gpsimd.dma_start(out=gain[:], in_=gn.rearrange("(p t) o -> p (t o)", t=PACK))
+        load_scale_rows([nc.gpsimd] * QUADS, w2_s, w2_scales)
+        nc.sync.dma_start(offs_sb[:], offs)
+        nc.sync.dma_start(out=w1_w[:], in_=as_words(w1_words))
+        load_scale_rows([nc.sync] * QUADS, x_s, x_scales)
+        nc.sync.dma_start(out=x_w[:], in_=as_words(x_words))
+        load_scale_rows([nc.sync] * QUADS, w1_s, w1_scales)
+        tab_rows = tab.rearrange("(p t) u -> p t u", t=PACK)
+        nc.sync.dma_start(out=tab_raw[0][:], in_=tab_rows[:, 0, :])
+        nc.sync.dma_start(nb_sb[:], nb)
+        nc.sync.dma_start(out=w2_w[:], in_=as_words(w2_words))
+        nc.sync.dma_start(kind_sb[:], kind)
+        for t in range(1, PACK):
+            nc.sync.dma_start(out=tab_raw[t][:], in_=tab_rows[:, t, :])
+        res_rows = res.rearrange("(p t) j -> p t j", t=PACK)
+        for c, n in enumerate(CHUNKS):
+            nc.sync.dma_start(out=res_sb[c][:], in_=res_rows[:, :, starts[c] : starts[c] + n])
+
+        nc.scalar.activation(out=gain_abs[:], in_=gain[:], func=ACT.Abs)
+
+        w1_wd = keep.tile([P, PACK, P], I32, name="w1_wd", align_bytes=64)
+        w1_sd = keep.tile([P, PACK, P], U8, name="w1_sd", align_bytes=64)
+        w2_wd = keep.tile([P, PACK, P], I32, name="w2_wd", align_bytes=64)
+        xg_s = keep.tile([P, S], U8, name="xg_s", align_bytes=64)
+
+        deal(nc, w1_wd, w1_w, 0, PACK)
+        nc.vector.tensor_copy(xg_s[:], x_s[:].indirect(offs_sb[:]))
+        xg_w = [keep.tile([P, HALF], I32, name="xg_w0", align_bytes=64)]
+        nc.vector.tensor_copy(xg_w[0][:].bitcast(U32), x_w[:].bitcast(U32).indirect(offs_sb[:, 0 : HALF // 16]))
+        deal(nc, w1_sd, w1_s, 0, PACK)
+        xg_w.append(keep.tile([P, HALF], I32, name="xg_w1", tag="early", align_bytes=64))
+        nc.vector.tensor_copy(xg_w[1][:].bitcast(U32), x_w[:].bitcast(U32).indirect(offs_sb[:, HALF // 16 : S // 16]))
+
+        y_win = [keep.tile([P, S], F32, name="y_win%d" % t) for t in range(PACK)]
+        y_own = [keep.tile([P, S], F32, name="y_own%d" % t) for t in range(PACK)]
+        th_win = [keep.tile([P, H], F32, name="th_win%d" % t) for t in range(PACK)]
+        late = []
+        for t in range(PACK):
+            nc.scalar.activation(out=th_win[t][:], in_=tab_raw[t][:], func=ACT.Copy, scale=gain_abs[:, t : t + 1])
+            for h in range(2):
+                cols = slice(h * HALF, (h + 1) * HALF)
+                acc = psum.tile([P, HALF], F32, name="acc", tag="bank")
+                nc.tensor.matmul_mx(
+                    out=acc[:],
+                    lhsT=w1_wd[:, t, :].bitcast(FP8X4),
+                    lhsT_scale=w1_sd[:, t, :],
+                    rhs=xg_w[h][:].bitcast(FP8X4),
+                    rhs_scale=xg_s[:, cols],
+                    start=True,
+                    stop=True,
+                )
+                nc.scalar.activation(out=y_win[t][:, cols], in_=acc[:], func=ACT.Copy, scale=gain[:, t : t + 1])
+                if h == 0:
+                    nc.scalar.activation(out=y_own[t][:, cols], in_=acc[:], func=ACT.Copy, scale=gain[:, t : t + 1])
+                else:
+                    late.append((t, cols, acc))
+        for t, cols, acc in late:
+            nc.scalar.activation(out=y_own[t][:, cols], in_=acc[:], func=ACT.Copy, scale=gain[:, t : t + 1])
+
+        deal(nc, w2_wd, w2_w, 0, PACK)
+        w2_sd = keep.tile([P, PACK, P], U8, name="w2_sd", tag="tab_raw3", align_bytes=64)
+        deal(nc, w2_sd, w2_s, 0, PACK)
+
+        out_rows = out_0.rearrange("(p t) j -> p t j", t=PACK)
+        out_words = as_words(out_1)
+        o_s = keep.tile([P, S], U8, name="o_s", align_bytes=64)
+        for c, n in enumerate(CHUNKS):
+            cols = slice(starts[c], starts[c] + n)
+            lst = slice(starts[c] // 16, (starts[c] + n) // 16)
+            e = keep.tile([P, PACK, n], F32, name="e%d" % c, tag="e")
+            a = keep.tile([P, PACK, n], F32, name="a%d" % c)
+            m = keep.tile([P, PACK, n], F32, name="m%d" % c)
+            for t in range(PACK):
+                nc.vector.tensor_tensor(e[:, t, :], y_win[t][:].indirect(nb_sb[:, lst]), y_own[t][:, cols], ALU.subtract)
+                nc.vector.tensor_tensor(a[:, t, :], th_win[t][:].indirect(kind_sb[:, lst]), e[:, t, :], ALU.add)
+            step = 256 // n
+            last = c == len(CHUNKS) - 1
+            if not last:
+                z = keep.tile([P, PACK, n], BF16, name="z%d" % c)
+            z_il = keep.tile([P, n, PACK], BF16, name="z_il%d" % c, align_bytes=64)
+            for t in range(0, PACK, step):
+                ts = slice(t, t + step)
+                nc.vector.scalar_tensor_tensor(
+                    out=m[:, ts, :], in0=e[:, ts, :], scalar=2.0, in1=a[:, ts, :], op0=ALU.mult, op1=ALU.max
+                )
+                if not last:
+                    nc.vector.scalar_tensor_tensor(
+                        out=z[:, ts, :], in0=a[:, ts, :], scalar=0.0, in1=m[:, ts, :], op0=ALU.max, op1=ALU.subtract
+                    )
+            if last:
+                nc.vector.scalar_tensor_tensor(
+                    out=z_il[:],
+                    in0=a[:].rearrange("p t j -> p j t"),
+                    scalar=0.0,
+                    in1=m[:].rearrange("p t j -> p j t"),
+                    op0=ALU.max,
+                    op1=ALU.subtract,
+                )
+            else:
+                nc.scalar.copy(out=z_il[:], in_=z[:].rearrange("p t j -> p j t"))
+            z_w = keep.tile([P, n], I32, name="z_w%d" % c, align_bytes=64)
+            nc.vector.quantize_mx(
+                out=z_w[:].bitcast(FP8X4), scales=z_s[:, cols], in_=z_il[:].rearrange("p j t -> p (j t)")
+            )
+            o = keep.tile([P, PACK, n], F32, name="o%d" % c)
+            per_bank = BANK // n
+            for t0 in range(0, PACK, per_bank):
+                acc = psum.tile([P, per_bank, n], F32, name="acc", tag="bank")
+                for t in range(t0, t0 + per_bank):
+                    nc.tensor.matmul_mx(
+                        out=acc[:, t - t0, :],
+                        lhsT=w2_wd[:, t, :].bitcast(FP8X4),
+                        lhsT_scale=w2_sd[:, t, :],
+                        rhs=z_w[:].bitcast(FP8X4),
+                        rhs_scale=z_s[:, cols],
+                        start=True,
+                        stop=True,
+                    )
+                ts = slice(t0, t0 + per_bank)
+                nc.vector.tensor_tensor(o[:, ts, :], acc[:], res_sb[c][:, ts, :], ALU.add)
+            nc.sync.dma_start(out=out_rows[:, :, cols], in_=o[:])
+            o_il = keep.tile([P, n, PACK], BF16, name="o_il%d" % c, align_bytes=64)
+            if last:
+                nc.vector.tensor_copy(out=o_il[:], in_=o[:].rearrange("p t j -> p j t"))
+            else:
+                nc.scalar.copy(out=o_il[:], in_=o[:].rearrange("p t j -> p j t"))
+            o_w = keep.tile([P, n], I32, name="o_w%d" % c, align_bytes=64)
+            nc.vector.quantize_mx(
+                out=o_w[:].bitcast(FP8X4), scales=o_s[:, cols], in_=o_il[:].rearrange("p j t -> p (j t)")
+            )
+            nc.sync.dma_start(out=out_words[:, cols], in_=o_w[:])
+        for q in range(QUADS):
+            queue = nc.sync if q % 2 == 0 else nc.scalar
+            queue.dma_start(out=out_2[0, 4 * q : 4 * q + 4, :].bitcast(I32), in_=o_s[32 * q : 32 * q + 4, :].bitcast(I32))

@@ -34,7 +34,7 @@ def load_scale_rows(queues, plane, scales):
 
 
 def deal(nc, dst, src, t0, t1):
-    nc.vector.tensor_copy(out=dst[:, t0:t1, :], in_=src[:].rearrange("p (m t) -> p t m", t=PACK)[:, t0:t1, :])
+    nc.vector.tensor_copy(out=dst[:], in_=src[:].rearrange("p (m t) -> p t m", t=PACK)[:, t0:t1, :])
 
 
 def tile_picked_softthr_none_po_kernel(
@@ -48,7 +48,7 @@ def tile_picked_softthr_none_po_kernel(
         offs_sb = keep.tile([P, S // 16], U16, name="offs_sb")
         kind_sb = keep.tile([P, S // 16], U16, name="kind_sb")
         nb_sb = keep.tile([P, S // 16], U16, name="nb_sb")
-        x_w = keep.tile([P, T], I32, name="x_w", align_bytes=64)
+        x_w = keep.tile([P, T], I32, name="x_w", tag="x_w", align_bytes=64)
         x_s = keep.tile([P, T], U8, name="x_s", align_bytes=64)
         w1_w = keep.tile([P, H], I32, name="w1_w", align_bytes=64)
         w1_s = keep.tile([P, H], U8, name="w1_s", tag="early", align_bytes=64)
@@ -65,8 +65,7 @@ def tile_picked_softthr_none_po_kernel(
         nc.vector.memset(w1_s[:].bitcast(I32), 0)
         nc.vector.memset(w2_s[:].bitcast(I32), 0)
         nc.vector.memset(z_s[:].bitcast(I32), 0)
-        nc.gpsimd.dma_start(out=gain[:], in_=gn.rearrange("(p t) o -> p (t o)", t=PACK))
-        load_scale_rows([nc.gpsimd] * QUADS, w2_s, w2_scales)
+        nc.scalar.dma_start(out=gain[:], in_=gn.rearrange("(p t) o -> p (t o)", t=PACK))
         nc.sync.dma_start(offs_sb[:], offs)
         nc.sync.dma_start(out=w1_w[:], in_=as_words(w1_words))
         load_scale_rows([nc.sync] * QUADS, x_s, x_scales)
@@ -78,6 +77,8 @@ def tile_picked_softthr_none_po_kernel(
         nc.sync.dma_start(out=w2_w[:], in_=as_words(w2_words))
         nc.sync.dma_start(kind_sb[:], kind)
         for t in range(1, PACK):
+            if t == PACK - 1:
+                load_scale_rows([nc.sync] * QUADS, w2_s, w2_scales)
             nc.sync.dma_start(out=tab_raw[t][:], in_=tab_rows[:, t, :])
         res_rows = res.rearrange("(p t) j -> p t j", t=PACK)
         for c, n in enumerate(CHUNKS):
@@ -85,75 +86,88 @@ def tile_picked_softthr_none_po_kernel(
 
         nc.scalar.activation(out=gain_abs[:], in_=gain[:], func=ACT.Abs)
 
-        w1_wd = keep.tile([P, PACK, P], I32, name="w1_wd", align_bytes=64)
+        w1_wd0 = keep.tile([P, 1, P], I32, name="w1_wd0", align_bytes=64)
         w1_sd = keep.tile([P, PACK, P], U8, name="w1_sd", align_bytes=64)
         w2_wd = keep.tile([P, PACK, P], I32, name="w2_wd", align_bytes=64)
+        w2_sd = keep.tile([P, PACK, P], U8, name="w2_sd", align_bytes=64)
         xg_s = keep.tile([P, S], U8, name="xg_s", align_bytes=64)
 
-        deal(nc, w1_wd, w1_w, 0, PACK)
+        deal(nc, w1_wd0, w1_w, 0, 1)
         nc.vector.tensor_copy(xg_s[:], x_s[:].indirect(offs_sb[:]))
         xg_w = [keep.tile([P, HALF], I32, name="xg_w0", align_bytes=64)]
         nc.vector.tensor_copy(xg_w[0][:].bitcast(U32), x_w[:].bitcast(U32).indirect(offs_sb[:, 0 : HALF // 16]))
         deal(nc, w1_sd, w1_s, 0, PACK)
         xg_w.append(keep.tile([P, HALF], I32, name="xg_w1", tag="early", align_bytes=64))
         nc.vector.tensor_copy(xg_w[1][:].bitcast(U32), x_w[:].bitcast(U32).indirect(offs_sb[:, HALF // 16 : S // 16]))
+        w1_wd1 = keep.tile([P, PACK - 1, P], I32, name="w1_wd1", tag="x_w", align_bytes=64)
+        deal(nc, w1_wd1, w1_w, 1, PACK)
+        w1_tiles = [w1_wd0[:, 0, :]] + [w1_wd1[:, t, :] for t in range(PACK - 1)]
 
         y_win = [keep.tile([P, S], F32, name="y_win%d" % t) for t in range(PACK)]
         y_own = [keep.tile([P, S], F32, name="y_own%d" % t) for t in range(PACK)]
         th_win = [keep.tile([P, H], F32, name="th_win%d" % t) for t in range(PACK)]
-        late = []
+        halves = [slice(h * HALF, (h + 1) * HALF) for h in range(2)]
         for t in range(PACK):
             nc.scalar.activation(out=th_win[t][:], in_=tab_raw[t][:], func=ACT.Copy, scale=gain_abs[:, t : t + 1])
+            if t == 0:
+                accs = [psum.tile([P, HALF], F32, name="acc", tag="bank") for h in range(2)]
+                outs = [acc[:] for acc in accs]
+                reads = [(halves[h], outs[h]) for h in range(2)]
+            else:
+                acc = psum.tile([P, S], F32, name="acc", tag="bank")
+                outs = [acc[:, cols] for cols in halves]
+                reads = [(slice(0, S), acc[:])]
             for h in range(2):
-                cols = slice(h * HALF, (h + 1) * HALF)
-                acc = psum.tile([P, HALF], F32, name="acc", tag="bank")
                 nc.tensor.matmul_mx(
-                    out=acc[:],
-                    lhsT=w1_wd[:, t, :].bitcast(FP8X4),
+                    out=outs[h],
+                    lhsT=w1_tiles[t].bitcast(FP8X4),
                     lhsT_scale=w1_sd[:, t, :],
                     rhs=xg_w[h][:].bitcast(FP8X4),
-                    rhs_scale=xg_s[:, cols],
+                    rhs_scale=xg_s[:, halves[h]],
                     start=True,
                     stop=True,
                 )
-                nc.scalar.activation(out=y_win[t][:, cols], in_=acc[:], func=ACT.Copy, scale=gain[:, t : t + 1])
-                if h == 0:
-                    nc.scalar.activation(out=y_own[t][:, cols], in_=acc[:], func=ACT.Copy, scale=gain[:, t : t + 1])
-                else:
-                    late.append((t, cols, acc))
-        for t, cols, acc in late:
-            nc.scalar.activation(out=y_own[t][:, cols], in_=acc[:], func=ACT.Copy, scale=gain[:, t : t + 1])
+            for dst in (y_win, y_own):
+                for cols, src in reads:
+                    nc.scalar.activation(out=dst[t][:, cols], in_=src, func=ACT.Copy, scale=gain[:, t : t + 1])
 
         deal(nc, w2_wd, w2_w, 0, PACK)
-        w2_sd = keep.tile([P, PACK, P], U8, name="w2_sd", tag="tab_raw3", align_bytes=64)
         deal(nc, w2_sd, w2_s, 0, PACK)
 
         out_rows = out_0.rearrange("(p t) j -> p t j", t=PACK)
         out_words = as_words(out_1)
         o_s = keep.tile([P, S], U8, name="o_s", align_bytes=64)
+        diffs = [keep.tile([P, PACK, n], F32, name="e%d" % c, tag="e%d" % c) for c, n in enumerate(CHUNKS)]
+
+        def differences(c, t):
+            cols = slice(starts[c], starts[c] + CHUNKS[c])
+            lst = slice(cols.start // 16, cols.stop // 16)
+            nc.vector.tensor_tensor(diffs[c][:, t, :], y_win[t][:].indirect(nb_sb[:, lst]), y_own[t][:, cols], ALU.subtract)
+
         for c, n in enumerate(CHUNKS):
             cols = slice(starts[c], starts[c] + n)
             lst = slice(starts[c] // 16, (starts[c] + n) // 16)
-            e = keep.tile([P, PACK, n], F32, name="e%d" % c, tag="e")
-            a = keep.tile([P, PACK, n], F32, name="a%d" % c)
+            e = diffs[c]
+            a = keep.tile([P, PACK, n], F32, name="a%d" % c, tag="e%d" % (c - 1))
             m = keep.tile([P, PACK, n], F32, name="m%d" % c)
-            for t in range(PACK):
-                nc.vector.tensor_tensor(e[:, t, :], y_win[t][:].indirect(nb_sb[:, lst]), y_own[t][:, cols], ALU.subtract)
-                nc.vector.tensor_tensor(a[:, t, :], th_win[t][:].indirect(kind_sb[:, lst]), e[:, t, :], ALU.add)
-            step = 256 // n
             last = c == len(CHUNKS) - 1
-            if not last:
-                z = keep.tile([P, PACK, n], BF16, name="z%d" % c)
-            z_il = keep.tile([P, n, PACK], BF16, name="z_il%d" % c, align_bytes=64)
-            for t in range(0, PACK, step):
-                ts = slice(t, t + step)
-                nc.vector.scalar_tensor_tensor(
-                    out=m[:, ts, :], in0=e[:, ts, :], scalar=2.0, in1=a[:, ts, :], op0=ALU.mult, op1=ALU.max
-                )
-                if not last:
+            for t in range(PACK):
+                if c == 0:
+                    differences(0, t)
+                nc.vector.tensor_tensor(a[:, t, :], th_win[t][:].indirect(kind_sb[:, lst]), e[:, t, :], ALU.add)
+                if c == 0:
                     nc.vector.scalar_tensor_tensor(
-                        out=z[:, ts, :], in0=a[:, ts, :], scalar=0.0, in1=m[:, ts, :], op0=ALU.max, op1=ALU.subtract
+                        out=m[:, t, :], in0=e[:, t, :], scalar=2.0, in1=a[:, t, :], op0=ALU.mult, op1=ALU.max
                     )
+                    for later in range(1, len(CHUNKS)):
+                        differences(later, t)
+            if c > 0:
+                for t in range(0, PACK, 2):
+                    ts = slice(t, t + 2)
+                    nc.vector.scalar_tensor_tensor(
+                        out=m[:, ts, :], in0=e[:, ts, :], scalar=2.0, in1=a[:, ts, :], op0=ALU.mult, op1=ALU.max
+                    )
+            z_il = keep.tile([P, n, PACK], BF16, name="z_il%d" % c, align_bytes=64)
             if last:
                 nc.vector.scalar_tensor_tensor(
                     out=z_il[:],
@@ -164,6 +178,13 @@ def tile_picked_softthr_none_po_kernel(
                     op1=ALU.subtract,
                 )
             else:
+                z = keep.tile([P, PACK, n], BF16, name="z%d" % c)
+                span = PACK if c == 0 else 2
+                for t in range(0, PACK, span):
+                    ts = slice(t, t + span)
+                    nc.vector.scalar_tensor_tensor(
+                        out=z[:, ts, :], in0=a[:, ts, :], scalar=0.0, in1=m[:, ts, :], op0=ALU.max, op1=ALU.subtract
+                    )
                 nc.scalar.copy(out=z_il[:], in_=z[:].rearrange("p t j -> p j t"))
             z_w = keep.tile([P, n], I32, name="z_w%d" % c, align_bytes=64)
             nc.vector.quantize_mx(

@@ -21,6 +21,7 @@ QUADS = 4
 HALF = S // 2
 CHUNKS = (256, 128, 128)
 BANK = 512
+EARLY = 2
 FLOPS = 2 * 2 * 512 * 512 * 512
 
 
@@ -33,8 +34,15 @@ def load_scale_rows(queues, plane, scales):
         queue.dma_start(out=plane[32 * q : 32 * q + 4, :].bitcast(I32), in_=scales[0, 4 * q : 4 * q + 4, :].bitcast(I32))
 
 
-def deal(nc, dst, src, t0, t1):
-    nc.vector.tensor_copy(out=dst[:], in_=src[:].rearrange("p (m t) -> p t m", t=PACK)[:, t0:t1, :])
+def deal(nc, dst, src, t0, t1, run):
+    nc.vector.tensor_copy(
+        out=dst[:].rearrange("p t (b i) -> p b t i", i=run),
+        in_=src[:].rearrange("p (b i t) -> p b t i", i=run, t=PACK)[:, :, t0:t1, :],
+    )
+
+
+def weave(copy, dst, src):
+    copy(out=dst[:].rearrange("p (b i) t -> p b t i", i=4), in_=src[:].rearrange("p t (b i) -> p b t i", i=4))
 
 
 def tile_picked_softthr_none_po_kernel(
@@ -48,98 +56,103 @@ def tile_picked_softthr_none_po_kernel(
         offs_sb = keep.tile([P, S // 16], U16, name="offs_sb")
         kind_sb = keep.tile([P, S // 16], U16, name="kind_sb")
         nb_sb = keep.tile([P, S // 16], U16, name="nb_sb")
-        x_w = keep.tile([P, T], I32, name="x_w", tag="x_w", align_bytes=64)
+        x_w = keep.tile([P, T], I32, name="x_w", align_bytes=64)
         x_s = keep.tile([P, T], U8, name="x_s", align_bytes=64)
         w1_w = keep.tile([P, H], I32, name="w1_w", align_bytes=64)
-        w1_s = keep.tile([P, H], U8, name="w1_s", tag="early", align_bytes=64)
+        w1_s = keep.tile([P, H], U8, name="w1_s", tag="w1_s", align_bytes=64)
         w2_w = keep.tile([P, H], I32, name="w2_w", align_bytes=64)
         w2_s = keep.tile([P, H], U8, name="w2_s", align_bytes=64)
         gain = keep.tile([P, PACK], F32, name="gain")
         gain_abs = keep.tile([P, PACK], F32, name="gain_abs")
-        tab_raw = [keep.tile([P, H], F32, name="tab_raw%d" % t, tag="tab_raw%d" % t, align_bytes=64) for t in range(PACK)]
+        gain_neg = keep.tile([P, PACK], F32, name="gain_neg")
+        tab_win = [keep.tile([P, H], F32, name="tab_win%d" % t, tag="tab%d" % t) for t in range(PACK)]
         res_sb = [keep.tile([P, PACK, n], F32, name="res_sb%d" % c) for c, n in enumerate(CHUNKS)]
         z_s = keep.tile([P, S], U8, name="z_s", align_bytes=64)
 
         starts = [sum(CHUNKS[:c]) for c in range(len(CHUNKS))]
+        halves = [slice(h * HALF, (h + 1) * HALF) for h in range(2)]
         nc.vector.memset(x_s[:].bitcast(I32), 0)
         nc.vector.memset(w1_s[:].bitcast(I32), 0)
         nc.vector.memset(w2_s[:].bitcast(I32), 0)
         nc.vector.memset(z_s[:].bitcast(I32), 0)
-        nc.scalar.dma_start(out=gain[:], in_=gn.rearrange("(p t) o -> p (t o)", t=PACK))
+        tab_rows = tab.rearrange("(p t) u -> p t u", t=PACK)
         nc.sync.dma_start(offs_sb[:], offs)
-        nc.sync.dma_start(out=w1_w[:], in_=as_words(w1_words))
+        nc.sync.dma_start(kind_sb[:], kind)
+        nc.sync.dma_start(out=tab_win[0][:], in_=tab_rows[:, 0, :])
         load_scale_rows([nc.sync] * QUADS, x_s, x_scales)
         nc.sync.dma_start(out=x_w[:], in_=as_words(x_words))
+        nc.sync.dma_start(out=w1_w[:], in_=as_words(w1_words))
         load_scale_rows([nc.sync] * QUADS, w1_s, w1_scales)
-        tab_rows = tab.rearrange("(p t) u -> p t u", t=PACK)
-        nc.sync.dma_start(out=tab_raw[0][:], in_=tab_rows[:, 0, :])
+        nc.sync.dma_start(out=gain[:], in_=gn.rearrange("(p t) o -> p (t o)", t=PACK))
+        nc.sync.dma_start(out=tab_win[1][:], in_=tab_rows[:, 1, :])
         nc.sync.dma_start(nb_sb[:], nb)
+        nc.sync.dma_start(out=tab_win[2][:], in_=tab_rows[:, 2, :])
         nc.sync.dma_start(out=w2_w[:], in_=as_words(w2_words))
-        nc.sync.dma_start(kind_sb[:], kind)
-        for t in range(1, PACK):
-            if t == PACK - 1:
-                load_scale_rows([nc.sync] * QUADS, w2_s, w2_scales)
-            nc.sync.dma_start(out=tab_raw[t][:], in_=tab_rows[:, t, :])
+        nc.sync.dma_start(out=tab_win[3][:], in_=tab_rows[:, 3, :])
+        load_scale_rows([nc.sync] * QUADS, w2_s, w2_scales)
         res_rows = res.rearrange("(p t) j -> p t j", t=PACK)
         for c, n in enumerate(CHUNKS):
             nc.sync.dma_start(out=res_sb[c][:], in_=res_rows[:, :, starts[c] : starts[c] + n])
 
         nc.scalar.activation(out=gain_abs[:], in_=gain[:], func=ACT.Abs)
+        nc.scalar.activation(out=gain_neg[:], in_=gain_abs[:], func=ACT.Copy, scale=-1.0)
+
+        th = [keep.tile([P, S], F32, name="th%d" % t) for t in range(EARLY)]
+
+        def thresholds(t, cols):
+            nc.vector.tensor_copy(th[t][:, cols], tab_win[t][:].indirect(kind_sb[:, cols.start // 16 : cols.stop // 16]))
 
         w1_wd0 = keep.tile([P, 1, P], I32, name="w1_wd0", align_bytes=64)
-        w1_sd = keep.tile([P, PACK, P], U8, name="w1_sd", align_bytes=64)
+        w1_sd0 = keep.tile([P, 1, P], U8, name="w1_sd0", align_bytes=64)
+        w1_sd1 = keep.tile([P, PACK - 1, P], U8, name="w1_sd1", align_bytes=64)
         w2_wd = keep.tile([P, PACK, P], I32, name="w2_wd", align_bytes=64)
         w2_sd = keep.tile([P, PACK, P], U8, name="w2_sd", align_bytes=64)
         xg_s = keep.tile([P, S], U8, name="xg_s", align_bytes=64)
+        xg_w = keep.tile([P, S], I32, name="xg_w", align_bytes=64)
 
-        deal(nc, w1_wd0, w1_w, 0, 1)
+        for cols in halves:
+            thresholds(0, cols)
         nc.vector.tensor_copy(xg_s[:], x_s[:].indirect(offs_sb[:]))
-        xg_w = [keep.tile([P, HALF], I32, name="xg_w0", align_bytes=64)]
-        nc.vector.tensor_copy(xg_w[0][:].bitcast(U32), x_w[:].bitcast(U32).indirect(offs_sb[:, 0 : HALF // 16]))
-        deal(nc, w1_sd, w1_s, 0, PACK)
-        xg_w.append(keep.tile([P, HALF], I32, name="xg_w1", tag="early", align_bytes=64))
-        nc.vector.tensor_copy(xg_w[1][:].bitcast(U32), x_w[:].bitcast(U32).indirect(offs_sb[:, HALF // 16 : S // 16]))
-        w1_wd1 = keep.tile([P, PACK - 1, P], I32, name="w1_wd1", tag="x_w", align_bytes=64)
-        deal(nc, w1_wd1, w1_w, 1, PACK)
-        w1_tiles = [w1_wd0[:, 0, :]] + [w1_wd1[:, t, :] for t in range(PACK - 1)]
+        nc.vector.tensor_copy(xg_w[:].bitcast(U32), x_w[:].bitcast(U32).indirect(offs_sb[:]))
+        deal(nc, w1_wd0, w1_w, 0, 1, 4)
+        deal(nc, w1_sd0, w1_s, 0, 1, 16)
+        deal(nc, w1_sd1, w1_s, 1, PACK, 16)
+        w1_wd1 = keep.tile([P, PACK - 1, P], I32, name="w1_wd1", tag="w1_s", align_bytes=64)
+        deal(nc, w1_wd1, w1_w, 1, PACK, 4)
+        w1_tiles = [(w1_wd0[:, 0, :], w1_sd0[:, 0, :])] + [(w1_wd1[:, t, :], w1_sd1[:, t, :]) for t in range(PACK - 1)]
+        for cols in halves:
+            thresholds(1, cols)
 
         y_win = [keep.tile([P, S], F32, name="y_win%d" % t) for t in range(PACK)]
         y_own = [keep.tile([P, S], F32, name="y_own%d" % t) for t in range(PACK)]
-        th_win = [keep.tile([P, H], F32, name="th_win%d" % t) for t in range(PACK)]
-        halves = [slice(h * HALF, (h + 1) * HALF) for h in range(2)]
+        scaled_win = {}
         for t in range(PACK):
-            nc.scalar.activation(out=th_win[t][:], in_=tab_raw[t][:], func=ACT.Copy, scale=gain_abs[:, t : t + 1])
-            if t == 0:
-                accs = [psum.tile([P, HALF], F32, name="acc", tag="bank") for h in range(2)]
-                outs = [acc[:] for acc in accs]
-                reads = [(halves[h], outs[h]) for h in range(2)]
-            else:
-                acc = psum.tile([P, S], F32, name="acc", tag="bank")
-                outs = [acc[:, cols] for cols in halves]
-                reads = [(slice(0, S), acc[:])]
-            for h in range(2):
+            if t >= EARLY:
+                scaled_win[t] = keep.tile([P, H], F32, name="scaled_win%d" % t, tag="tab%d" % (t - 1))
+                nc.scalar.activation(out=scaled_win[t][:], in_=tab_win[t][:], func=ACT.Copy, scale=gain_abs[:, t : t + 1])
+            for cols in halves if t == 0 else [slice(0, S)]:
+                acc = psum.tile([P, cols.stop - cols.start], F32, name="acc", tag="bank")
                 nc.tensor.matmul_mx(
-                    out=outs[h],
-                    lhsT=w1_tiles[t].bitcast(FP8X4),
-                    lhsT_scale=w1_sd[:, t, :],
-                    rhs=xg_w[h][:].bitcast(FP8X4),
-                    rhs_scale=xg_s[:, halves[h]],
+                    out=acc[:],
+                    lhsT=w1_tiles[t][0].bitcast(FP8X4),
+                    lhsT_scale=w1_tiles[t][1],
+                    rhs=xg_w[:, cols].bitcast(FP8X4),
+                    rhs_scale=xg_s[:, cols],
                     start=True,
                     stop=True,
                 )
-            for dst in (y_win, y_own):
-                for cols, src in reads:
-                    nc.scalar.activation(out=dst[t][:, cols], in_=src, func=ACT.Copy, scale=gain[:, t : t + 1])
-
-        deal(nc, w2_wd, w2_w, 0, PACK)
-        deal(nc, w2_sd, w2_s, 0, PACK)
+                nc.scalar.activation(out=y_win[t][:, cols], in_=acc[:], func=ACT.Copy, scale=gain[:, t : t + 1])
+                nc.scalar.activation(out=y_own[t][:, cols], in_=acc[:], func=ACT.Copy, scale=gain[:, t : t + 1])
 
         out_rows = out_0.rearrange("(p t) j -> p t j", t=PACK)
         out_words = as_words(out_1)
         o_s = keep.tile([P, S], U8, name="o_s", align_bytes=64)
-        diffs = [keep.tile([P, PACK, n], F32, name="e%d" % c, tag="e%d" % c) for c, n in enumerate(CHUNKS)]
+        tags = {"e": ["x", "z", "w"], "a": ["y", "x", "z"], "m": ["w", "y", "x"]}
+        diffs = {}
 
         def differences(c, t):
+            if c not in diffs:
+                diffs[c] = keep.tile([P, PACK, CHUNKS[c]], F32, name="e%d" % c, tag=tags["e"][c])
             cols = slice(starts[c], starts[c] + CHUNKS[c])
             lst = slice(cols.start // 16, cols.stop // 16)
             nc.vector.tensor_tensor(diffs[c][:, t, :], y_win[t][:].indirect(nb_sb[:, lst]), y_own[t][:, cols], ALU.subtract)
@@ -147,51 +160,49 @@ def tile_picked_softthr_none_po_kernel(
         for c, n in enumerate(CHUNKS):
             cols = slice(starts[c], starts[c] + n)
             lst = slice(starts[c] // 16, (starts[c] + n) // 16)
-            e = diffs[c]
-            a = keep.tile([P, PACK, n], F32, name="a%d" % c, tag="e%d" % (c - 1))
-            m = keep.tile([P, PACK, n], F32, name="m%d" % c)
             last = c == len(CHUNKS) - 1
+            a = keep.tile([P, PACK, n], F32, name="a%d" % c, tag=tags["a"][c])
+            m = keep.tile([P, PACK, n], F32, name="m%d" % c, tag=tags["m"][c])
+            z = keep.tile([P, PACK, n], BF16, name="z%d" % c)
             for t in range(PACK):
-                if c == 0:
-                    differences(0, t)
-                nc.vector.tensor_tensor(a[:, t, :], th_win[t][:].indirect(kind_sb[:, lst]), e[:, t, :], ALU.add)
-                if c == 0:
+                if c != 1:
+                    differences(c, t)
+                e = diffs[c]
+                if t < EARLY:
+                    nc.vector.scalar_tensor_tensor(
+                        out=a[:, t, :], in0=th[t][:, cols], scalar=gain_abs[:, t : t + 1], in1=e[:, t, :], op0=ALU.mult, op1=ALU.max
+                    )
+                    nc.vector.scalar_tensor_tensor(
+                        out=m[:, t, :], in0=th[t][:, cols], scalar=gain_neg[:, t : t + 1], in1=e[:, t, :], op0=ALU.mult, op1=ALU.min
+                    )
+                    if t == EARLY - 1:
+                        ts = slice(0, EARLY)
+                        nc.vector.scalar_tensor_tensor(
+                            out=z[:, ts, :], in0=a[:, ts, :], scalar=-1.0, in1=m[:, ts, :], op0=ALU.mult, op1=ALU.subtract
+                        )
+                else:
+                    nc.vector.tensor_tensor(a[:, t, :], scaled_win[t][:].indirect(kind_sb[:, lst]), e[:, t, :], ALU.add)
                     nc.vector.scalar_tensor_tensor(
                         out=m[:, t, :], in0=e[:, t, :], scalar=2.0, in1=a[:, t, :], op0=ALU.mult, op1=ALU.max
                     )
-                    for later in range(1, len(CHUNKS)):
-                        differences(later, t)
-            if c > 0:
-                for t in range(0, PACK, 2):
-                    ts = slice(t, t + 2)
-                    nc.vector.scalar_tensor_tensor(
-                        out=m[:, ts, :], in0=e[:, ts, :], scalar=2.0, in1=a[:, ts, :], op0=ALU.mult, op1=ALU.max
-                    )
+                    if last or t == PACK - 1:
+                        ts = slice(t if last else EARLY, t + 1)
+                        nc.vector.scalar_tensor_tensor(
+                            out=z[:, ts, :], in0=a[:, ts, :], scalar=0.0, in1=m[:, ts, :], op0=ALU.max, op1=ALU.subtract
+                        )
+                if c == 0:
+                    differences(1, t)
+            if c == 0:
+                deal(nc, w2_wd, w2_w, 0, PACK, 4)
+                deal(nc, w2_sd, w2_s, 0, PACK, 16)
             z_il = keep.tile([P, n, PACK], BF16, name="z_il%d" % c, align_bytes=64)
-            if last:
-                nc.vector.scalar_tensor_tensor(
-                    out=z_il[:],
-                    in0=a[:].rearrange("p t j -> p j t"),
-                    scalar=0.0,
-                    in1=m[:].rearrange("p t j -> p j t"),
-                    op0=ALU.max,
-                    op1=ALU.subtract,
-                )
-            else:
-                z = keep.tile([P, PACK, n], BF16, name="z%d" % c)
-                span = PACK if c == 0 else 2
-                for t in range(0, PACK, span):
-                    ts = slice(t, t + span)
-                    nc.vector.scalar_tensor_tensor(
-                        out=z[:, ts, :], in0=a[:, ts, :], scalar=0.0, in1=m[:, ts, :], op0=ALU.max, op1=ALU.subtract
-                    )
-                nc.scalar.copy(out=z_il[:], in_=z[:].rearrange("p t j -> p j t"))
+            weave(nc.vector.tensor_copy if last else nc.scalar.copy, z_il, z)
             z_w = keep.tile([P, n], I32, name="z_w%d" % c, align_bytes=64)
             nc.vector.quantize_mx(
                 out=z_w[:].bitcast(FP8X4), scales=z_s[:, cols], in_=z_il[:].rearrange("p j t -> p (j t)")
             )
             o = keep.tile([P, PACK, n], F32, name="o%d" % c)
-            per_bank = BANK // n
+            per_bank = 2 if last else BANK // n
             for t0 in range(0, PACK, per_bank):
                 acc = psum.tile([P, per_bank, n], F32, name="acc", tag="bank")
                 for t in range(t0, t0 + per_bank):
@@ -208,10 +219,7 @@ def tile_picked_softthr_none_po_kernel(
                 nc.vector.tensor_tensor(o[:, ts, :], acc[:], res_sb[c][:, ts, :], ALU.add)
             nc.sync.dma_start(out=out_rows[:, :, cols], in_=o[:])
             o_il = keep.tile([P, n, PACK], BF16, name="o_il%d" % c, align_bytes=64)
-            if last:
-                nc.vector.tensor_copy(out=o_il[:], in_=o[:].rearrange("p t j -> p j t"))
-            else:
-                nc.scalar.copy(out=o_il[:], in_=o[:].rearrange("p t j -> p j t"))
+            weave(nc.vector.tensor_copy if last else nc.scalar.copy, o_il, o)
             o_w = keep.tile([P, n], I32, name="o_w%d" % c, align_bytes=64)
             nc.vector.quantize_mx(
                 out=o_w[:].bitcast(FP8X4), scales=o_s[:, cols], in_=o_il[:].rearrange("p j t -> p (j t)")

@@ -1,6 +1,7 @@
 from contextlib import ExitStack
 
 import concourse.mybir as mybir
+from concourse.masks import make_identity
 
 F32 = mybir.dt.float32
 BF16 = mybir.dt.bfloat16
@@ -14,24 +15,41 @@ ACT = mybir.ActivationFunctionType
 
 P = 128
 PACK = 4
-T = 2048
+TOKENS = 2048
 S = 512
 H = 512
-QUADS = 4
+GROUP = 16
+QUADRANT = 32
+SCALE_ROWS = 4
 HALF = S // 2
-CHUNKS = (256, 128, 128)
 BANK = 512
+LINE_WORDS = 4
+LINE_BYTES = 16
+MX_ALIGN = 64
+CHUNKS = (256, 128, 128)
 EARLY = 2
-FLOPS = 2 * 2 * 512 * 512 * 512
+FLOPS = 2 * (2 * 512 * H * S)
 
 
 def as_words(words):
     return words[0].rearrange("p n t -> p (n t)").bitcast(I32)
 
 
-def load_scale_rows(queues, plane, scales):
-    for q, queue in enumerate(queues):
-        queue.dma_start(out=plane[32 * q : 32 * q + 4, :].bitcast(I32), in_=scales[0, 4 * q : 4 * q + 4, :].bitcast(I32))
+def live_rows(plane, q):
+    return plane[QUADRANT * q : QUADRANT * q + SCALE_ROWS, :].bitcast(I32)
+
+
+def scale_rows(scales, q):
+    return scales[0, SCALE_ROWS * q : SCALE_ROWS * (q + 1), :].bitcast(I32)
+
+
+def load_scales(nc, plane, scales):
+    for q in range(P // QUADRANT):
+        nc.sync.dma_start(out=live_rows(plane, q), in_=scale_rows(scales, q))
+
+
+def entries(cols):
+    return slice(cols.start // GROUP, cols.stop // GROUP)
 
 
 def deal(nc, dst, src, t0, t1, run):
@@ -42,7 +60,53 @@ def deal(nc, dst, src, t0, t1, run):
 
 
 def weave(copy, dst, src):
-    copy(out=dst[:].rearrange("p (b i) t -> p b t i", i=4), in_=src[:].rearrange("p t (b i) -> p b t i", i=4))
+    copy(
+        out=dst[:].rearrange("p (b i) t -> p b t i", i=LINE_WORDS),
+        in_=src[:].rearrange("p t (b i) -> p b t i", i=LINE_WORDS),
+    )
+
+
+def product(nc, out, weights, weight_scales, moving, moving_scales):
+    nc.tensor.matmul_mx(
+        out=out,
+        lhsT=weights.bitcast(FP8X4),
+        lhsT_scale=weight_scales,
+        rhs=moving.bitcast(FP8X4),
+        rhs_scale=moving_scales,
+        start=True,
+        stop=True,
+    )
+
+
+def quantise(nc, words, scales, woven):
+    nc.vector.quantize_mx(out=words[:].bitcast(FP8X4), scales=scales, in_=woven[:].rearrange("p j t -> p (j t)"))
+
+
+def fused(nc, out, in0, scalar, in1, op0, op1):
+    nc.vector.scalar_tensor_tensor(out=out, in0=in0, scalar=scalar, in1=in1, op0=op0, op1=op1)
+
+
+def sum_on_tensor_engine(nc, keep, psum, ident, left, right, z_woven):
+    n = z_woven.shape[1]
+    pairs = psum.tile([P, 2, n], F32, name="pairs", tag="bank")
+    blocks = [slice(j0, j0 + P) for j0 in range(0, n, P)]
+    turned = [psum.tile([P, PACK, P], F32, name="turned", tag="bank") for block in blocks]
+    for t in range(PACK):
+        for b, block in enumerate(blocks):
+            nc.tensor.matmul(turned[b][:, t, :], left[t][:, block], ident[:], is_transpose=True, start=True, stop=False)
+            nc.tensor.matmul(turned[b][:, t, :], right[t][:, block], ident[:], is_transpose=True, start=False, stop=True)
+    for b, block in enumerate(blocks):
+        rounded = keep.tile([P, 2, P, 2], BF16, name="rounded%d" % b, align_bytes=MX_ALIGN)
+        nc.scalar.activation(
+            out=rounded[:], in_=turned[b][:].rearrange("j (u v) p -> j u p v", v=2), func=ACT.Copy, scale=-1.0
+        )
+        rounded_words = rounded[:].rearrange("j u p v -> j (u p v)").bitcast(F32)
+        for u in range(2):
+            nc.tensor.transpose(pairs[:, u, block], rounded_words[:, u * P : (u + 1) * P], ident[:])
+    nc.scalar.copy(
+        out=z_woven[:].rearrange("p j t -> p (j t)").bitcast(F32).rearrange("p (j u) -> p j u", u=2),
+        in_=pairs[:].rearrange("p u j -> p j u"),
+    )
 
 
 def tile_picked_softthr_none_po_kernel(
@@ -53,178 +117,172 @@ def tile_picked_softthr_none_po_kernel(
         keep = ctx.enter_context(tc.tile_pool(name="keep", bufs=1))
         psum = ctx.enter_context(tc.psum_pool(name="psum", bufs=8))
 
-        offs_sb = keep.tile([P, S // 16], U16, name="offs_sb")
-        kind_sb = keep.tile([P, S // 16], U16, name="kind_sb")
-        nb_sb = keep.tile([P, S // 16], U16, name="nb_sb")
-        x_w = keep.tile([P, T], I32, name="x_w", align_bytes=64)
-        x_s = keep.tile([P, T], U8, name="x_s", align_bytes=64)
-        w1_w = keep.tile([P, H], I32, name="w1_w", align_bytes=64)
-        w1_s = keep.tile([P, H], U8, name="w1_s", tag="w1_s", align_bytes=64)
-        w2_w = keep.tile([P, H], I32, name="w2_w", align_bytes=64)
-        w2_s = keep.tile([P, H], U8, name="w2_s", align_bytes=64)
+        offs_sb = keep.tile([P, S // GROUP], U16, name="offs_sb")
+        kind_sb = keep.tile([P, S // GROUP], U16, name="kind_sb")
+        nb_sb = keep.tile([P, S // GROUP], U16, name="nb_sb")
+        x_w = keep.tile([P, TOKENS], I32, name="x_w", align_bytes=MX_ALIGN)
+        x_s = keep.tile([P, TOKENS], U8, name="x_s", align_bytes=MX_ALIGN)
+        w1_w = keep.tile([P, H], I32, name="w1_w", tag="w1_w", align_bytes=MX_ALIGN)
+        w1_s = keep.tile([P, H], U8, name="w1_s", tag="w1_s", align_bytes=MX_ALIGN)
+        w2_w = keep.tile([P, H], I32, name="w2_w", align_bytes=MX_ALIGN)
+        w2_s = keep.tile([P, H], U8, name="w2_s", align_bytes=MX_ALIGN)
         gain = keep.tile([P, PACK], F32, name="gain")
         gain_abs = keep.tile([P, PACK], F32, name="gain_abs")
+        gain_abs_neg = keep.tile([P, PACK], F32, name="gain_abs_neg")
         gain_neg = keep.tile([P, PACK], F32, name="gain_neg")
         tab_win = [keep.tile([P, H], F32, name="tab_win%d" % t, tag="tab%d" % t) for t in range(PACK)]
         res_sb = [keep.tile([P, PACK, n], F32, name="res_sb%d" % c) for c, n in enumerate(CHUNKS)]
-        z_s = keep.tile([P, S], U8, name="z_s", align_bytes=64)
+        z_s = keep.tile([P, S], U8, name="z_s", align_bytes=MX_ALIGN)
 
-        starts = [sum(CHUNKS[:c]) for c in range(len(CHUNKS))]
+        chunk_cols = [slice(sum(CHUNKS[:c]), sum(CHUNKS[: c + 1])) for c in range(len(CHUNKS))]
         halves = [slice(h * HALF, (h + 1) * HALF) for h in range(2)]
-        nc.vector.memset(x_s[:].bitcast(I32), 0)
-        nc.vector.memset(w1_s[:].bitcast(I32), 0)
-        nc.vector.memset(w2_s[:].bitcast(I32), 0)
-        nc.vector.memset(z_s[:].bitcast(I32), 0)
+
+        for plane in (x_s, w1_s, w2_s, z_s):
+            nc.vector.memset(plane[:].bitcast(I32), 0)
+
         tab_rows = tab.rearrange("(p t) u -> p t u", t=PACK)
         nc.sync.dma_start(offs_sb[:], offs)
         nc.sync.dma_start(kind_sb[:], kind)
         nc.sync.dma_start(out=tab_win[0][:], in_=tab_rows[:, 0, :])
-        load_scale_rows([nc.sync] * QUADS, x_s, x_scales)
+        load_scales(nc, x_s, x_scales)
         nc.sync.dma_start(out=x_w[:], in_=as_words(x_words))
         nc.sync.dma_start(out=w1_w[:], in_=as_words(w1_words))
-        load_scale_rows([nc.sync] * QUADS, w1_s, w1_scales)
+        load_scales(nc, w1_s, w1_scales)
         nc.sync.dma_start(out=gain[:], in_=gn.rearrange("(p t) o -> p (t o)", t=PACK))
         nc.sync.dma_start(out=tab_win[1][:], in_=tab_rows[:, 1, :])
         nc.sync.dma_start(nb_sb[:], nb)
         nc.sync.dma_start(out=tab_win[2][:], in_=tab_rows[:, 2, :])
         nc.sync.dma_start(out=w2_w[:], in_=as_words(w2_words))
         nc.sync.dma_start(out=tab_win[3][:], in_=tab_rows[:, 3, :])
-        load_scale_rows([nc.sync] * QUADS, w2_s, w2_scales)
+        load_scales(nc, w2_s, w2_scales)
         res_rows = res.rearrange("(p t) j -> p t j", t=PACK)
-        for c, n in enumerate(CHUNKS):
-            nc.sync.dma_start(out=res_sb[c][:], in_=res_rows[:, :, starts[c] : starts[c] + n])
+        for c, cols in enumerate(chunk_cols):
+            nc.sync.dma_start(out=res_sb[c][:], in_=res_rows[:, :, cols])
 
+        nc.scalar.activation(out=gain_neg[:], in_=gain[:], func=ACT.Copy, scale=-1.0)
         nc.scalar.activation(out=gain_abs[:], in_=gain[:], func=ACT.Abs)
-        nc.scalar.activation(out=gain_neg[:], in_=gain_abs[:], func=ACT.Copy, scale=-1.0)
+        nc.scalar.activation(out=gain_abs_neg[:], in_=gain_abs[:], func=ACT.Copy, scale=-1.0)
 
         th = [keep.tile([P, S], F32, name="th%d" % t) for t in range(EARLY)]
 
-        def thresholds(t, cols):
-            nc.vector.tensor_copy(th[t][:, cols], tab_win[t][:].indirect(kind_sb[:, cols.start // 16 : cols.stop // 16]))
+        def gather_thresholds(t):
+            for cols in halves:
+                nc.vector.tensor_copy(th[t][:, cols], tab_win[t][:].indirect(kind_sb[:, entries(cols)]))
 
-        w1_wd0 = keep.tile([P, 1, P], I32, name="w1_wd0", align_bytes=64)
-        w1_sd0 = keep.tile([P, 1, P], U8, name="w1_sd0", align_bytes=64)
-        w1_sd1 = keep.tile([P, PACK - 1, P], U8, name="w1_sd1", align_bytes=64)
-        w2_wd = keep.tile([P, PACK, P], I32, name="w2_wd", align_bytes=64)
-        w2_sd = keep.tile([P, PACK, P], U8, name="w2_sd", align_bytes=64)
-        xg_s = keep.tile([P, S], U8, name="xg_s", align_bytes=64)
-        xg_w = keep.tile([P, S], I32, name="xg_w", align_bytes=64)
+        w1_w_head = keep.tile([P, 1, P], I32, name="w1_w_head", align_bytes=MX_ALIGN)
+        w1_s_head = keep.tile([P, 1, P], U8, name="w1_s_head", align_bytes=MX_ALIGN)
+        w1_s_rest = keep.tile([P, PACK - 1, P], U8, name="w1_s_rest", align_bytes=MX_ALIGN)
+        w2_w_dealt = keep.tile([P, PACK, P], I32, name="w2_w_dealt", align_bytes=MX_ALIGN)
+        w2_s_dealt = keep.tile([P, PACK, P], U8, name="w2_s_dealt", align_bytes=MX_ALIGN)
+        picked_s = keep.tile([P, S], U8, name="picked_s", align_bytes=MX_ALIGN)
+        picked_w = keep.tile([P, S], I32, name="picked_w", align_bytes=MX_ALIGN)
 
-        for cols in halves:
-            thresholds(0, cols)
-        nc.vector.tensor_copy(xg_s[:], x_s[:].indirect(offs_sb[:]))
-        nc.vector.tensor_copy(xg_w[:].bitcast(U32), x_w[:].bitcast(U32).indirect(offs_sb[:]))
-        deal(nc, w1_wd0, w1_w, 0, 1, 4)
-        deal(nc, w1_sd0, w1_s, 0, 1, 16)
-        deal(nc, w1_sd1, w1_s, 1, PACK, 16)
-        w1_wd1 = keep.tile([P, PACK - 1, P], I32, name="w1_wd1", tag="w1_s", align_bytes=64)
-        deal(nc, w1_wd1, w1_w, 1, PACK, 4)
-        w1_tiles = [(w1_wd0[:, 0, :], w1_sd0[:, 0, :])] + [(w1_wd1[:, t, :], w1_sd1[:, t, :]) for t in range(PACK - 1)]
-        for cols in halves:
-            thresholds(1, cols)
+        gather_thresholds(0)
+        nc.vector.tensor_copy(picked_s[:], x_s[:].indirect(offs_sb[:]))
+        nc.vector.tensor_copy(picked_w[:].bitcast(U32), x_w[:].bitcast(U32).indirect(offs_sb[:]))
+        deal(nc, w1_w_head, w1_w, 0, 1, LINE_WORDS)
+        deal(nc, w1_s_head, w1_s, 0, 1, LINE_BYTES)
+        deal(nc, w1_s_rest, w1_s, 1, PACK, LINE_BYTES)
+        w1_w_rest = keep.tile([P, PACK - 1, P], I32, name="w1_w_rest", tag="w1_s", align_bytes=MX_ALIGN)
+        deal(nc, w1_w_rest, w1_w, 1, PACK, LINE_WORDS)
+        w1_dealt = [(w1_w_head[:, 0, :], w1_s_head[:, 0, :])]
+        w1_dealt.extend((w1_w_rest[:, t, :], w1_s_rest[:, t, :]) for t in range(PACK - 1))
+        ident = keep.tile([P, P], F32, name="ident", tag="w1_w", align_bytes=MX_ALIGN)
+        make_identity(nc, ident[:])
+        gather_thresholds(1)
 
         y_win = [keep.tile([P, S], F32, name="y_win%d" % t) for t in range(PACK)]
         y_own = [keep.tile([P, S], F32, name="y_own%d" % t) for t in range(PACK)]
-        scaled_win = {}
+        neg_tab_win = {}
         for t in range(PACK):
             if t >= EARLY:
-                scaled_win[t] = keep.tile([P, H], F32, name="scaled_win%d" % t, tag="tab%d" % (t - 1))
-                nc.scalar.activation(out=scaled_win[t][:], in_=tab_win[t][:], func=ACT.Copy, scale=gain_abs[:, t : t + 1])
+                neg_tab_win[t] = keep.tile([P, H], F32, name="neg_tab_win%d" % t, tag="tab%d" % (t - 1))
+                nc.scalar.activation(out=neg_tab_win[t][:], in_=tab_win[t][:], func=ACT.Copy, scale=gain_abs_neg[:, t : t + 1])
+            row_factor = (gain if t < EARLY else gain_neg)[:, t : t + 1]
             for cols in halves if t == 0 else [slice(0, S)]:
-                acc = psum.tile([P, cols.stop - cols.start], F32, name="acc", tag="bank")
-                nc.tensor.matmul_mx(
-                    out=acc[:],
-                    lhsT=w1_tiles[t][0].bitcast(FP8X4),
-                    lhsT_scale=w1_tiles[t][1],
-                    rhs=xg_w[:, cols].bitcast(FP8X4),
-                    rhs_scale=xg_s[:, cols],
-                    start=True,
-                    stop=True,
-                )
-                nc.scalar.activation(out=y_win[t][:, cols], in_=acc[:], func=ACT.Copy, scale=gain[:, t : t + 1])
-                nc.scalar.activation(out=y_own[t][:, cols], in_=acc[:], func=ACT.Copy, scale=gain[:, t : t + 1])
+                y_acc = psum.tile([P, cols.stop - cols.start], F32, name="y_acc", tag="bank")
+                product(nc, y_acc[:], w1_dealt[t][0], w1_dealt[t][1], picked_w[:, cols], picked_s[:, cols])
+                nc.scalar.activation(out=y_win[t][:, cols], in_=y_acc[:], func=ACT.Copy, scale=row_factor)
+                nc.scalar.activation(out=y_own[t][:, cols], in_=y_acc[:], func=ACT.Copy, scale=row_factor)
 
         out_rows = out_0.rearrange("(p t) j -> p t j", t=PACK)
         out_words = as_words(out_1)
-        o_s = keep.tile([P, S], U8, name="o_s", align_bytes=64)
-        tags = {"e": ["x", "z", "w"], "a": ["y", "x", "z"], "m": ["w", "y", "x"]}
+        out_s = keep.tile([P, S], U8, name="out_s", align_bytes=MX_ALIGN)
+
+        e_bytes = ("e0", "e1", "second0")
+        first_bytes = ("first0", "e0", "z_woven0")
+        second_bytes = ("second0", "first0", "e0")
         diffs = {}
 
-        def differences(c, t):
+        def gather_differences(c, t):
             if c not in diffs:
-                diffs[c] = keep.tile([P, PACK, CHUNKS[c]], F32, name="e%d" % c, tag=tags["e"][c])
-            cols = slice(starts[c], starts[c] + CHUNKS[c])
-            lst = slice(cols.start // 16, cols.stop // 16)
-            nc.vector.tensor_tensor(diffs[c][:, t, :], y_win[t][:].indirect(nb_sb[:, lst]), y_own[t][:, cols], ALU.subtract)
+                diffs[c] = keep.tile([P, PACK, CHUNKS[c]], F32, name="e%d" % c, tag=e_bytes[c], align_bytes=MX_ALIGN)
+            cols = chunk_cols[c]
+            nc.vector.tensor_tensor(
+                diffs[c][:, t, :], y_win[t][:].indirect(nb_sb[:, entries(cols)]), y_own[t][:, cols], ALU.subtract
+            )
 
         for c, n in enumerate(CHUNKS):
-            cols = slice(starts[c], starts[c] + n)
-            lst = slice(starts[c] // 16, (starts[c] + n) // 16)
+            cols = chunk_cols[c]
+            opening = c == 0
             last = c == len(CHUNKS) - 1
-            a = keep.tile([P, PACK, n], F32, name="a%d" % c, tag=tags["a"][c])
-            m = keep.tile([P, PACK, n], F32, name="m%d" % c, tag=tags["m"][c])
-            z = keep.tile([P, PACK, n], BF16, name="z%d" % c)
+            first = keep.tile([P, PACK, n], F32, name="first%d" % c, tag=first_bytes[c], align_bytes=MX_ALIGN)
+            second = keep.tile([P, PACK, n], F32, name="second%d" % c, tag=second_bytes[c], align_bytes=MX_ALIGN)
+            if opening:
+                relu_part = keep.tile([P, PACK - EARLY, n], F32, name="relu_part")
+            else:
+                z = keep.tile([P, PACK, n], BF16, name="z%d" % c)
             for t in range(PACK):
-                if c != 1:
-                    differences(c, t)
-                e = diffs[c]
+                if opening or last:
+                    gather_differences(c, t)
+                e = diffs[c][:, t, :]
                 if t < EARLY:
-                    nc.vector.scalar_tensor_tensor(
-                        out=a[:, t, :], in0=th[t][:, cols], scalar=gain_abs[:, t : t + 1], in1=e[:, t, :], op0=ALU.mult, op1=ALU.max
-                    )
-                    nc.vector.scalar_tensor_tensor(
-                        out=m[:, t, :], in0=th[t][:, cols], scalar=gain_neg[:, t : t + 1], in1=e[:, t, :], op0=ALU.mult, op1=ALU.min
-                    )
-                    if t == EARLY - 1:
-                        ts = slice(0, EARLY)
-                        nc.vector.scalar_tensor_tensor(
-                            out=z[:, ts, :], in0=a[:, ts, :], scalar=-1.0, in1=m[:, ts, :], op0=ALU.mult, op1=ALU.subtract
-                        )
+                    fused(nc, first[:, t, :], th[t][:, cols], gain_abs[:, t : t + 1], e, ALU.mult, ALU.max)
+                    fused(nc, second[:, t, :], th[t][:, cols], gain_abs_neg[:, t : t + 1], e, ALU.mult, ALU.min)
+                    if not opening and t == EARLY - 1:
+                        fused(nc, z[:, :EARLY, :], first[:, :EARLY, :], -1.0, second[:, :EARLY, :], ALU.mult, ALU.subtract)
                 else:
-                    nc.vector.tensor_tensor(a[:, t, :], scaled_win[t][:].indirect(kind_sb[:, lst]), e[:, t, :], ALU.add)
-                    nc.vector.scalar_tensor_tensor(
-                        out=m[:, t, :], in0=e[:, t, :], scalar=2.0, in1=a[:, t, :], op0=ALU.mult, op1=ALU.max
+                    nc.vector.tensor_tensor(
+                        first[:, t, :], neg_tab_win[t][:].indirect(kind_sb[:, entries(cols)]), e, ALU.subtract
                     )
-                    if last or t == PACK - 1:
+                    fused(nc, second[:, t, :], e, -2.0, first[:, t, :], ALU.mult, ALU.min)
+                    if opening:
+                        nc.scalar.activation(out=relu_part[:, t - EARLY, :], in_=first[:, t, :], func=ACT.Relu, scale=-1.0)
+                    elif last or t == PACK - 1:
                         ts = slice(t if last else EARLY, t + 1)
-                        nc.vector.scalar_tensor_tensor(
-                            out=z[:, ts, :], in0=a[:, ts, :], scalar=0.0, in1=m[:, ts, :], op0=ALU.max, op1=ALU.subtract
-                        )
-                if c == 0:
-                    differences(1, t)
-            if c == 0:
-                deal(nc, w2_wd, w2_w, 0, PACK, 4)
-                deal(nc, w2_sd, w2_s, 0, PACK, 16)
-            z_il = keep.tile([P, n, PACK], BF16, name="z_il%d" % c, align_bytes=64)
-            weave(nc.vector.tensor_copy if last else nc.scalar.copy, z_il, z)
-            z_w = keep.tile([P, n], I32, name="z_w%d" % c, align_bytes=64)
-            nc.vector.quantize_mx(
-                out=z_w[:].bitcast(FP8X4), scales=z_s[:, cols], in_=z_il[:].rearrange("p j t -> p (j t)")
-            )
-            o = keep.tile([P, PACK, n], F32, name="o%d" % c)
-            per_bank = 2 if last else BANK // n
+                        fused(nc, z[:, ts, :], first[:, ts, :], 0.0, second[:, ts, :], ALU.min, ALU.subtract)
+                if opening:
+                    gather_differences(c + 1, t)
+            if opening:
+                deal(nc, w2_w_dealt, w2_w, 0, PACK, LINE_WORDS)
+                deal(nc, w2_s_dealt, w2_s, 0, PACK, LINE_BYTES)
+
+            weaver = nc.vector.tensor_copy if last else nc.scalar.copy
+            z_woven = keep.tile([P, n, PACK], BF16, name="z_woven%d" % c, tag="z_woven%d" % c, align_bytes=MX_ALIGN)
+            if opening:
+                addends = [first[:, t, :] if t < EARLY else relu_part[:, t - EARLY, :] for t in range(PACK)]
+                sum_on_tensor_engine(nc, keep, psum, ident, [second[:, t, :] for t in range(PACK)], addends, z_woven)
+            else:
+                weave(weaver, z_woven, z)
+            z_w = keep.tile([P, n], I32, name="z_w%d" % c, align_bytes=MX_ALIGN)
+            quantise(nc, z_w, z_s[:, cols], z_woven)
+
+            result = keep.tile([P, PACK, n], F32, name="result%d" % c)
+            per_bank = PACK // 2 if last else BANK // n
             for t0 in range(0, PACK, per_bank):
-                acc = psum.tile([P, per_bank, n], F32, name="acc", tag="bank")
+                out_acc = psum.tile([P, per_bank, n], F32, name="out_acc", tag="bank")
                 for t in range(t0, t0 + per_bank):
-                    nc.tensor.matmul_mx(
-                        out=acc[:, t - t0, :],
-                        lhsT=w2_wd[:, t, :].bitcast(FP8X4),
-                        lhsT_scale=w2_sd[:, t, :],
-                        rhs=z_w[:].bitcast(FP8X4),
-                        rhs_scale=z_s[:, cols],
-                        start=True,
-                        stop=True,
-                    )
+                    product(nc, out_acc[:, t - t0, :], w2_w_dealt[:, t, :], w2_s_dealt[:, t, :], z_w[:], z_s[:, cols])
                 ts = slice(t0, t0 + per_bank)
-                nc.vector.tensor_tensor(o[:, ts, :], acc[:], res_sb[c][:, ts, :], ALU.add)
-            nc.sync.dma_start(out=out_rows[:, :, cols], in_=o[:])
-            o_il = keep.tile([P, n, PACK], BF16, name="o_il%d" % c, align_bytes=64)
-            weave(nc.vector.tensor_copy if last else nc.scalar.copy, o_il, o)
-            o_w = keep.tile([P, n], I32, name="o_w%d" % c, align_bytes=64)
-            nc.vector.quantize_mx(
-                out=o_w[:].bitcast(FP8X4), scales=o_s[:, cols], in_=o_il[:].rearrange("p j t -> p (j t)")
-            )
-            nc.sync.dma_start(out=out_words[:, cols], in_=o_w[:])
-        for q in range(QUADS):
+                nc.vector.tensor_tensor(result[:, ts, :], out_acc[:], res_sb[c][:, ts, :], ALU.add)
+            nc.sync.dma_start(out=out_rows[:, :, cols], in_=result[:])
+
+            result_woven = keep.tile([P, n, PACK], BF16, name="result_woven%d" % c, align_bytes=MX_ALIGN)
+            weave(weaver, result_woven, result)
+            out_w = keep.tile([P, n], I32, name="out_w%d" % c, align_bytes=MX_ALIGN)
+            quantise(nc, out_w, out_s[:, cols], result_woven)
+            nc.sync.dma_start(out=out_words[:, cols], in_=out_w[:])
+
+        for q in range(P // QUADRANT):
             queue = nc.sync if q % 2 == 0 else nc.scalar
-            queue.dma_start(out=out_2[0, 4 * q : 4 * q + 4, :].bitcast(I32), in_=o_s[32 * q : 32 * q + 4, :].bitcast(I32))
+            queue.dma_start(out=scale_rows(out_2, q), in_=live_rows(out_s, q))

from contextlib import ExitStack

import concourse.mybir as mybir
from concourse.masks import make_identity

F32 = mybir.dt.float32
BF16 = mybir.dt.bfloat16
I32 = mybir.dt.int32
U32 = mybir.dt.uint32
U16 = mybir.dt.uint16
U8 = mybir.dt.uint8
FP8X4 = mybir.dt.float8_e4m3fn_x4
ALU = mybir.AluOpType
ACT = mybir.ActivationFunctionType

P = 128
PACK = 4
TOKENS = 2048
S = 512
H = 512
GROUP = 16
QUADRANT = 32
SCALE_ROWS = 4
HALF = S // 2
BANK = 512
LINE_WORDS = 4
LINE_BYTES = 16
MX_ALIGN = 64
CHUNKS = (256, 128, 128)
EARLY = 2
FLOPS = 2 * (2 * 512 * H * S)


def as_words(words):
    return words[0].rearrange("p n t -> p (n t)").bitcast(I32)


def live_rows(plane, q):
    return plane[QUADRANT * q : QUADRANT * q + SCALE_ROWS, :].bitcast(I32)


def scale_rows(scales, q):
    return scales[0, SCALE_ROWS * q : SCALE_ROWS * (q + 1), :].bitcast(I32)


def load_scales(nc, plane, scales):
    for q in range(P // QUADRANT):
        nc.sync.dma_start(out=live_rows(plane, q), in_=scale_rows(scales, q))


def entries(cols):
    return slice(cols.start // GROUP, cols.stop // GROUP)


def deal(nc, dst, src, t0, t1, run):
    nc.vector.tensor_copy(
        out=dst[:].rearrange("p t (b i) -> p b t i", i=run),
        in_=src[:].rearrange("p (b i t) -> p b t i", i=run, t=PACK)[:, :, t0:t1, :],
    )


def weave(copy, dst, src):
    copy(
        out=dst[:].rearrange("p (b i) t -> p b t i", i=LINE_WORDS),
        in_=src[:].rearrange("p t (b i) -> p b t i", i=LINE_WORDS),
    )


def product(nc, out, weights, weight_scales, moving, moving_scales):
    nc.tensor.matmul_mx(
        out=out,
        lhsT=weights.bitcast(FP8X4),
        lhsT_scale=weight_scales,
        rhs=moving.bitcast(FP8X4),
        rhs_scale=moving_scales,
        start=True,
        stop=True,
    )


def quantise(nc, words, scales, woven):
    nc.vector.quantize_mx(out=words[:].bitcast(FP8X4), scales=scales, in_=woven[:].rearrange("p j t -> p (j t)"))


def fused(nc, out, in0, scalar, in1, op0, op1):
    nc.vector.scalar_tensor_tensor(out=out, in0=in0, scalar=scalar, in1=in1, op0=op0, op1=op1)


def sum_on_tensor_engine(nc, keep, psum, ident, left, right, z_woven):
    n = z_woven.shape[1]
    pairs = psum.tile([P, 2, n], F32, name="pairs", tag="bank")
    blocks = [slice(j0, j0 + P) for j0 in range(0, n, P)]
    turned = [psum.tile([P, PACK, P], F32, name="turned", tag="bank") for block in blocks]
    for t in range(PACK):
        for b, block in enumerate(blocks):
            nc.tensor.matmul(turned[b][:, t, :], left[t][:, block], ident[:], is_transpose=True, start=True, stop=False)
            nc.tensor.matmul(turned[b][:, t, :], right[t][:, block], ident[:], is_transpose=True, start=False, stop=True)
    for b, block in enumerate(blocks):
        rounded = keep.tile([P, 2, P, 2], BF16, name="rounded%d" % b, align_bytes=MX_ALIGN)
        nc.scalar.activation(
            out=rounded[:], in_=turned[b][:].rearrange("j (u v) p -> j u p v", v=2), func=ACT.Copy, scale=-1.0
        )
        rounded_words = rounded[:].rearrange("j u p v -> j (u p v)").bitcast(F32)
        for u in range(2):
            nc.tensor.transpose(pairs[:, u, block], rounded_words[:, u * P : (u + 1) * P], ident[:])
    nc.scalar.copy(
        out=z_woven[:].rearrange("p j t -> p (j t)").bitcast(F32).rearrange("p (j u) -> p j u", u=2),
        in_=pairs[:].rearrange("p u j -> p j u"),
    )


def tile_picked_softthr_none_po_kernel(
    tc, x_words, x_scales, w1_words, w1_scales, tab, gn, w2_words, w2_scales, res, offs, kind, nb, out_0, out_1, out_2
):
    nc = tc.nc
    with ExitStack() as ctx:
        keep = ctx.enter_context(tc.tile_pool(name="keep", bufs=1))
        psum = ctx.enter_context(tc.psum_pool(name="psum", bufs=8))

        offs_sb = keep.tile([P, S // GROUP], U16, name="offs_sb")
        kind_sb = keep.tile([P, S // GROUP], U16, name="kind_sb")
        nb_sb = keep.tile([P, S // GROUP], U16, name="nb_sb")
        x_w = keep.tile([P, TOKENS], I32, name="x_w", align_bytes=MX_ALIGN)
        x_s = keep.tile([P, TOKENS], U8, name="x_s", align_bytes=MX_ALIGN)
        w1_w = keep.tile([P, H], I32, name="w1_w", tag="w1_w", align_bytes=MX_ALIGN)
        w1_s = keep.tile([P, H], U8, name="w1_s", tag="w1_s", align_bytes=MX_ALIGN)
        w2_w = keep.tile([P, H], I32, name="w2_w", align_bytes=MX_ALIGN)
        w2_s = keep.tile([P, H], U8, name="w2_s", align_bytes=MX_ALIGN)
        gain = keep.tile([P, PACK], F32, name="gain")
        gain_abs = keep.tile([P, PACK], F32, name="gain_abs")
        gain_abs_neg = keep.tile([P, PACK], F32, name="gain_abs_neg")
        gain_neg = keep.tile([P, PACK], F32, name="gain_neg")
        tab_win = [keep.tile([P, H], F32, name="tab_win%d" % t, tag="tab%d" % t) for t in range(PACK)]
        res_sb = [keep.tile([P, PACK, n], F32, name="res_sb%d" % c) for c, n in enumerate(CHUNKS)]
        z_s = keep.tile([P, S], U8, name="z_s", align_bytes=MX_ALIGN)

        chunk_cols = [slice(sum(CHUNKS[:c]), sum(CHUNKS[: c + 1])) for c in range(len(CHUNKS))]
        halves = [slice(h * HALF, (h + 1) * HALF) for h in range(2)]

        for plane in (x_s, w1_s, w2_s, z_s):
            nc.vector.memset(plane[:].bitcast(I32), 0)

        tab_rows = tab.rearrange("(p t) u -> p t u", t=PACK)
        nc.sync.dma_start(offs_sb[:], offs)
        nc.sync.dma_start(kind_sb[:], kind)
        nc.sync.dma_start(out=tab_win[0][:], in_=tab_rows[:, 0, :])
        load_scales(nc, x_s, x_scales)
        nc.sync.dma_start(out=x_w[:], in_=as_words(x_words))
        nc.sync.dma_start(out=w1_w[:], in_=as_words(w1_words))
        load_scales(nc, w1_s, w1_scales)
        nc.sync.dma_start(out=gain[:], in_=gn.rearrange("(p t) o -> p (t o)", t=PACK))
        nc.sync.dma_start(out=tab_win[1][:], in_=tab_rows[:, 1, :])
        nc.sync.dma_start(nb_sb[:], nb)
        nc.sync.dma_start(out=tab_win[2][:], in_=tab_rows[:, 2, :])
        nc.sync.dma_start(out=w2_w[:], in_=as_words(w2_words))
        nc.sync.dma_start(out=tab_win[3][:], in_=tab_rows[:, 3, :])
        load_scales(nc, w2_s, w2_scales)
        res_rows = res.rearrange("(p t) j -> p t j", t=PACK)
        for c, cols in enumerate(chunk_cols):
            nc.sync.dma_start(out=res_sb[c][:], in_=res_rows[:, :, cols])

        nc.scalar.activation(out=gain_neg[:], in_=gain[:], func=ACT.Copy, scale=-1.0)
        nc.scalar.activation(out=gain_abs[:], in_=gain[:], func=ACT.Abs)
        nc.scalar.activation(out=gain_abs_neg[:], in_=gain_abs[:], func=ACT.Copy, scale=-1.0)

        th = [keep.tile([P, S], F32, name="th%d" % t) for t in range(EARLY)]

        def gather_thresholds(t):
            for cols in halves:
                nc.vector.tensor_copy(th[t][:, cols], tab_win[t][:].indirect(kind_sb[:, entries(cols)]))

        w1_w_head = keep.tile([P, 1, P], I32, name="w1_w_head", align_bytes=MX_ALIGN)
        w1_s_head = keep.tile([P, 1, P], U8, name="w1_s_head", align_bytes=MX_ALIGN)
        w1_s_rest = keep.tile([P, PACK - 1, P], U8, name="w1_s_rest", align_bytes=MX_ALIGN)
        w2_w_dealt = keep.tile([P, PACK, P], I32, name="w2_w_dealt", align_bytes=MX_ALIGN)
        w2_s_dealt = keep.tile([P, PACK, P], U8, name="w2_s_dealt", align_bytes=MX_ALIGN)
        picked_s = keep.tile([P, S], U8, name="picked_s", align_bytes=MX_ALIGN)
        picked_w = keep.tile([P, S], I32, name="picked_w", align_bytes=MX_ALIGN)

        gather_thresholds(0)
        nc.vector.tensor_copy(picked_s[:], x_s[:].indirect(offs_sb[:]))
        nc.vector.tensor_copy(picked_w[:].bitcast(U32), x_w[:].bitcast(U32).indirect(offs_sb[:]))
        deal(nc, w1_w_head, w1_w, 0, 1, LINE_WORDS)
        deal(nc, w1_s_head, w1_s, 0, 1, LINE_BYTES)
        deal(nc, w1_s_rest, w1_s, 1, PACK, LINE_BYTES)
        w1_w_rest = keep.tile([P, PACK - 1, P], I32, name="w1_w_rest", tag="w1_s", align_bytes=MX_ALIGN)
        deal(nc, w1_w_rest, w1_w, 1, PACK, LINE_WORDS)
        w1_dealt = [(w1_w_head[:, 0, :], w1_s_head[:, 0, :])]
        w1_dealt.extend((w1_w_rest[:, t, :], w1_s_rest[:, t, :]) for t in range(PACK - 1))
        ident = keep.tile([P, P], F32, name="ident", tag="w1_w", align_bytes=MX_ALIGN)
        make_identity(nc, ident[:])
        gather_thresholds(1)

        y_win = [keep.tile([P, S], F32, name="y_win%d" % t) for t in range(PACK)]
        y_own = [keep.tile([P, S], F32, name="y_own%d" % t) for t in range(PACK)]
        neg_tab_win = {}
        for t in range(PACK):
            if t >= EARLY:
                neg_tab_win[t] = keep.tile([P, H], F32, name="neg_tab_win%d" % t, tag="tab%d" % (t - 1))
                nc.scalar.activation(out=neg_tab_win[t][:], in_=tab_win[t][:], func=ACT.Copy, scale=gain_abs_neg[:, t : t + 1])
            row_factor = (gain if t < EARLY else gain_neg)[:, t : t + 1]
            for cols in halves if t == 0 else [slice(0, S)]:
                y_acc = psum.tile([P, cols.stop - cols.start], F32, name="y_acc", tag="bank")
                product(nc, y_acc[:], w1_dealt[t][0], w1_dealt[t][1], picked_w[:, cols], picked_s[:, cols])
                nc.scalar.activation(out=y_win[t][:, cols], in_=y_acc[:], func=ACT.Copy, scale=row_factor)
                nc.scalar.activation(out=y_own[t][:, cols], in_=y_acc[:], func=ACT.Copy, scale=row_factor)

        out_rows = out_0.rearrange("(p t) j -> p t j", t=PACK)
        out_words = as_words(out_1)
        out_s = keep.tile([P, S], U8, name="out_s", align_bytes=MX_ALIGN)

        e_bytes = ("e0", "e1", "second0")
        first_bytes = ("first0", "e0", "z_woven0")
        second_bytes = ("second0", "first0", "e0")
        diffs = {}

        def gather_differences(c, t):
            if c not in diffs:
                diffs[c] = keep.tile([P, PACK, CHUNKS[c]], F32, name="e%d" % c, tag=e_bytes[c], align_bytes=MX_ALIGN)
            cols = chunk_cols[c]
            nc.vector.tensor_tensor(
                diffs[c][:, t, :], y_win[t][:].indirect(nb_sb[:, entries(cols)]), y_own[t][:, cols], ALU.subtract
            )

        for c, n in enumerate(CHUNKS):
            cols = chunk_cols[c]
            opening = c == 0
            last = c == len(CHUNKS) - 1
            first = keep.tile([P, PACK, n], F32, name="first%d" % c, tag=first_bytes[c], align_bytes=MX_ALIGN)
            second = keep.tile([P, PACK, n], F32, name="second%d" % c, tag=second_bytes[c], align_bytes=MX_ALIGN)
            if opening:
                relu_part = keep.tile([P, PACK - EARLY, n], F32, name="relu_part")
            else:
                z = keep.tile([P, PACK, n], BF16, name="z%d" % c)
            for t in range(PACK):
                if opening or last:
                    gather_differences(c, t)
                e = diffs[c][:, t, :]
                if t < EARLY:
                    fused(nc, first[:, t, :], th[t][:, cols], gain_abs[:, t : t + 1], e, ALU.mult, ALU.max)
                    fused(nc, second[:, t, :], th[t][:, cols], gain_abs_neg[:, t : t + 1], e, ALU.mult, ALU.min)
                    if not opening and t == EARLY - 1:
                        fused(nc, z[:, :EARLY, :], first[:, :EARLY, :], -1.0, second[:, :EARLY, :], ALU.mult, ALU.subtract)
                else:
                    nc.vector.tensor_tensor(
                        first[:, t, :], neg_tab_win[t][:].indirect(kind_sb[:, entries(cols)]), e, ALU.subtract
                    )
                    fused(nc, second[:, t, :], e, -2.0, first[:, t, :], ALU.mult, ALU.min)
                    if opening:
                        nc.scalar.activation(out=relu_part[:, t - EARLY, :], in_=first[:, t, :], func=ACT.Relu, scale=-1.0)
                    elif last or t == PACK - 1:
                        ts = slice(t if last else EARLY, t + 1)
                        fused(nc, z[:, ts, :], first[:, ts, :], 0.0, second[:, ts, :], ALU.min, ALU.subtract)
                if opening:
                    gather_differences(c + 1, t)
            if opening:
                deal(nc, w2_w_dealt, w2_w, 0, PACK, LINE_WORDS)
                deal(nc, w2_s_dealt, w2_s, 0, PACK, LINE_BYTES)

            weaver = nc.vector.tensor_copy if last else nc.scalar.copy
            z_woven = keep.tile([P, n, PACK], BF16, name="z_woven%d" % c, tag="z_woven%d" % c, align_bytes=MX_ALIGN)
            if opening:
                addends = [first[:, t, :] if t < EARLY else relu_part[:, t - EARLY, :] for t in range(PACK)]
                sum_on_tensor_engine(nc, keep, psum, ident, [second[:, t, :] for t in range(PACK)], addends, z_woven)
            else:
                weave(weaver, z_woven, z)
            z_w = keep.tile([P, n], I32, name="z_w%d" % c, align_bytes=MX_ALIGN)
            quantise(nc, z_w, z_s[:, cols], z_woven)

            result = keep.tile([P, PACK, n], F32, name="result%d" % c)
            per_bank = PACK // 2 if last else BANK // n
            for t0 in range(0, PACK, per_bank):
                out_acc = psum.tile([P, per_bank, n], F32, name="out_acc", tag="bank")
                for t in range(t0, t0 + per_bank):
                    product(nc, out_acc[:, t - t0, :], w2_w_dealt[:, t, :], w2_s_dealt[:, t, :], z_w[:], z_s[:, cols])
                ts = slice(t0, t0 + per_bank)
                nc.vector.tensor_tensor(result[:, ts, :], out_acc[:], res_sb[c][:, ts, :], ALU.add)
            nc.sync.dma_start(out=out_rows[:, :, cols], in_=result[:])

            result_woven = keep.tile([P, n, PACK], BF16, name="result_woven%d" % c, align_bytes=MX_ALIGN)
            weave(weaver, result_woven, result)
            out_w = keep.tile([P, n], I32, name="out_w%d" % c, align_bytes=MX_ALIGN)
            quantise(nc, out_w, out_s[:, cols], result_woven)
            nc.sync.dma_start(out=out_words[:, cols], in_=out_w[:])

        for q in range(P // QUADRANT):
            queue = nc.sync if q % 2 == 0 else nc.scalar
            queue.dma_start(out=scale_rows(out_2, q), in_=live_rows(out_s, q))
